import numpy as np
import ml_dtypes


def mxq(x, axis, fmt="e4m3"):
    dtype, down = {"e4m3": (ml_dtypes.float8_e4m3fn, 7), "e5m2": (ml_dtypes.float8_e5m2, 14)}[fmt]
    v = np.moveaxis(np.asarray(x, np.float32).astype(ml_dtypes.bfloat16).astype(np.float64), axis, -1)
    blocks = v.reshape(v.shape[:-1] + (-1, 32))
    amax = np.abs(blocks).max(-1, keepdims=True)
    byte = np.maximum(np.where(amax > 0, np.frexp(amax)[1] - 1 + 127, 0) - down, 1)
    scale = np.exp2(byte - 127.0)
    codes = (blocks / scale).astype(np.float32).astype(dtype).astype(np.float64)
    return np.moveaxis((codes * scale).reshape(v.shape), -1, axis)


WIDE = False


def mx_kscale(k):
    if not WIDE:
        return np.ones(k)
    levels = np.array([30, -30])
    if k % 512:
        return np.exp2(np.random.permutation(np.resize(levels, k // 32))).repeat(32)
    a = np.empty((k // 512, 16))
    for p in range(k // 512):
        a[p, :8] = np.random.permutation(np.resize(levels, 8))
        for g in range(8):
            far = levels[np.abs(levels - a[p, g]) >= 10]
            a[p, g + 8] = far[np.random.randint(len(far))]
    return np.exp2(a.ravel()).repeat(32)


def f64(x):
    return np.asarray(x).astype(np.float64)


def striped(idx):
    return np.tile(np.asarray(idx).reshape(-1, 16).T, (8, 1)).astype(np.uint16)


def unstriped(offs):
    return offs[:16].T.reshape(-1).astype(np.int64)


E2M1 = np.array([0.0, 0.5, 1.0, 1.5, 2.0, 3.0, 4.0, 6.0, -0.0, -0.5, -1.0, -1.5, -2.0, -3.0, -4.0, -6.0])


def pack_weight(w, fmt):
    k, n = w.shape
    w = f64(np.asarray(w, np.float32).astype(ml_dtypes.bfloat16)).reshape(k // 32, 32, n)
    amax = np.abs(w).max(1)
    if fmt in ("e4m3", "e5m2"):
        byte = np.frexp(amax)[1] - 1 + 127 - (7 if fmt == "e4m3" else 14)
    else:
        mant, ex = np.frexp(amax / 6.0)
        byte = np.where(mant > 0.5, ex, ex - 1) + 127
    byte = np.clip(np.where(amax > 0, byte, 1), 1, 254)
    scaled = (w * np.exp2(127.0 - byte)[:, None, :]).reshape(k, n).astype(np.float32)
    by_word = np.ascontiguousarray(scaled.reshape(k // 512, 128, 4, n).transpose(0, 1, 3, 2))
    if fmt in ("e4m3", "e5m2"):
        words = by_word.astype(ml_dtypes.float8_e4m3fn if fmt == "e4m3" else ml_dtypes.float8_e5m2).view(np.uint8)
    else:
        c = by_word.astype(ml_dtypes.float4_e2m1fn).view(np.uint8) & 0xF
        words = (c[..., 0::2] | (c[..., 1::2] << 4)).reshape(k // 512, 128, 2 * n)
    return np.ascontiguousarray(words), np.ascontiguousarray(byte.astype(np.uint8).reshape(k // 512, 16, n))


def unpack_weight(words, scales, fmt):
    g, _, n = scales.shape
    words = np.ascontiguousarray(words).reshape(g, 128, n, -1)
    if fmt in ("e4m3", "e5m2"):
        vals = words.view(ml_dtypes.float8_e4m3fn if fmt == "e4m3" else ml_dtypes.float8_e5m2).astype(np.float64)
    else:
        nib = np.empty((g, 128, n, 4), np.uint8)
        nib[..., 0::2] = words & 0xF
        nib[..., 1::2] = words >> 4
        vals = E2M1[nib]
    vals = vals * np.repeat(np.exp2(scales.astype(np.float64) - 127.0), 8, axis=1)[..., None]
    return vals.transpose(0, 1, 3, 2).reshape(g * 512, n)


K, T, J, I, V, C = 1024, 1024, 256, 256, 1024, 512


def setup_inputs():
    n = np.random.standard_normal
    idx = np.random.permutation(T)[:J]
    idx2 = np.random.permutation(V)[:I]
    idx3 = np.random.permutation(C)[:I]
    fk = mx_kscale(K)
    xtp = pack_weight(n((K, T)) * 0.04 * fk[:, None], "e5m2")
    return {
        "xt_words": xtp[0],
        "xt_scales": xtp[1],
        "kf": (n((K, V))).astype(np.float32),
        "ko": (n((K, I)) * 0.6).astype(np.float32),
        "fi": (np.random.uniform(0.5, 2.0, (K, 1)) / fk[:, None]).astype(np.float32),
        "bi": (np.random.uniform(-0.7, 0.7, (1, I))).astype(np.float32),
        "tb": (1.0 * n((J, C))).astype(np.float32),
        "offs": striped(idx),
        "offs2": striped(idx2),
        "offs3": striped(idx3),
    }


def reference(xt_words, xt_scales, kf, ko, fi, bi, tb, offs, offs2, offs3):
    idx = unstriped(offs)
    idx2 = unstriped(offs2)
    idx3 = unstriped(offs3)
    xtu = unpack_weight(xt_words, xt_scales, "e5m2")
    vk = (f64(kf)[:, idx2] + f64(ko)) * f64(fi)
    xtidxg = xtu[:, idx]
    vkq = mxq(vk, 0, "e5m2")
    a0 = xtidxg.T @ vkq
    a = a0 + f64(bi)
    y = np.tanh(a) * f64(tb)[:, idx3]
    return y

@@ -1,0 +1,141 @@
+from contextlib import ExitStack
+
+import concourse.mybir as mybir
+from concourse.masks import make_identity
+
+K, T, J, I, V, C = 1024, 1024, 256, 256, 1024, 512
+FLOPS = 2 * K * J * I
+
+F32 = mybir.dt.float32
+BF16 = mybir.dt.bfloat16
+I32 = mybir.dt.int32
+U32 = mybir.dt.uint32
+U16 = mybir.dt.uint16
+U8 = mybir.dt.uint8
+E5M2X4 = mybir.dt.float8_e5m2_x4
+ADD = mybir.AluOpType.add
+MULT = mybir.AluOpType.mult
+COPY = mybir.ActivationFunctionType.Copy
+TANH = mybir.ActivationFunctionType.Tanh
+
+P = 128
+PACK = 4
+PASSES = K // (P * PACK)
+ROW_TILES = J // P
+LIST_COLS = J // 16
+
+
+def tile_list_scores_picked_mixed_tabled_kernel(
+    tc, xt_words, xt_scales, kf, ko, fi, bi, tb, offs, offs2, offs3, out
+):
+    nc = tc.nc
+    with ExitStack() as ctx:
+        keep = ctx.enter_context(tc.tile_pool(name="keep", bufs=1))
+        psum = ctx.enter_context(tc.psum_pool(name="psum", bufs=1))
+
+        tok_list = keep.tile([P, LIST_COLS], U16, name="tok_list")
+        key_list = keep.tile([P, LIST_COLS], U16, name="key_list")
+        fac_list = keep.tile([P, LIST_COLS], U16, name="fac_list")
+
+        kf_planes = kf.rearrange("(z p t) v -> z t p v", z=PASSES, t=PACK)
+        ko_rows = ko.rearrange("(z p t) i -> z p (t i)", z=PASSES, t=PACK)
+        store_keys = [
+            [keep.tile([P, V], F32, name=f"store_keys{z}{t}") for t in range(PACK)] for z in range(PASSES)
+        ]
+        own_keys = [keep.tile([P, PACK * I], F32, name=f"own_keys{z}") for z in range(PASSES)]
+        tok_words = [keep.tile([P, T], U32, name=f"tok_words{z}") for z in range(PASSES)]
+        factors = [keep.tile([P, C], F32, name=f"factors{h}") for h in range(ROW_TILES)]
+        feat = keep.tile([P, PASSES * PACK], F32, name="feat")
+        bias_col = keep.tile([P, 2], F32, name="bias_col")
+        tok_bytes = keep.tile([P, PASSES * T], U8, name="tok_bytes")
+
+        nc.scalar.dma_start(
+            out=feat[:].rearrange("p (z t) -> p z t", z=PASSES),
+            in_=fi.rearrange("(z p t) o -> p z (t o)", z=PASSES, t=PACK),
+        )
+        nc.vector.memset(tok_bytes[:].bitcast(I32), 0)
+
+        def load_scale_rows(q):
+            nc.sync.dma_start(
+                out=tok_bytes[32 * q : 32 * q + 4, :].bitcast(I32).rearrange("r (z c) -> r z c", z=PASSES),
+                in_=xt_scales[:, 4 * q : 4 * q + 4, :].bitcast(I32).rearrange("z r c -> r z c"),
+            )
+
+        small = [lambda q=q: load_scale_rows(q) for q in range(4)] + [
+            lambda: nc.sync.dma_start(tok_list[:], offs),
+            lambda: nc.sync.dma_start(out=bias_col[:], in_=bi.rearrange("o (p u) -> p (o u)", u=2)),
+            lambda: nc.sync.dma_start(fac_list[:], offs3),
+        ]
+        for z in range(PASSES):
+            for t in range(PACK):
+                nc.sync.dma_start(out=store_keys[z][t][:], in_=kf_planes[z, t])
+                if z == 0 and t == 0:
+                    nc.sync.dma_start(key_list[:], offs2)
+                else:
+                    small[z * PACK + t - 1]()
+                if t == 0:
+                    nc.sync.dma_start(out=own_keys[z][:], in_=ko_rows[z])
+        for z in range(PASSES):
+            nc.sync.dma_start(
+                out=tok_words[z][:].bitcast(I32),
+                in_=xt_words[z].rearrange("p c r -> p (c r)").bitcast(I32),
+            )
+        for h in range(ROW_TILES):
+            nc.sync.dma_start(out=factors[h][:], in_=tb[h * P : (h + 1) * P, :])
+
+        ident = keep.tile([P, P], F32, name="ident")
+        make_identity(nc, ident[:])
+
+        bias_ps = psum.tile([P, 2, P], F32, name="bias_ps")
+        for u in range(2):
+            nc.tensor.transpose(bias_ps[:, u, :], bias_col[:, u : u + 1].to_broadcast([P, P]), ident[:])
+        bias = keep.tile([P, I], F32, name="bias")
+        nc.scalar.copy(out=bias[:].rearrange("m (p u) -> m p u", u=2), in_=bias_ps[:].rearrange("m u p -> m p u"))
+
+        tok_scales = [keep.tile([P, J], U8, name=f"tok_scales{z}", align_bytes=64) for z in range(PASSES)]
+        for z in range(PASSES):
+            nc.vector.tensor_copy(tok_scales[z][:], tok_bytes[:, z * T : (z + 1) * T].indirect(tok_list[:]))
+
+        key_codes = [keep.tile([P, I], U32, name=f"key_codes{z}", align_bytes=64) for z in range(PASSES)]
+        key_scales = [keep.tile([P, I], U8, name=f"key_scales{z}", align_bytes=64) for z in range(PASSES)]
+        for z in range(PASSES):
+            grouped = keep.tile([P, I, PACK], BF16, name=f"grouped{z}", align_bytes=64)
+            for t in range(PACK):
+                summed = keep.tile([P, I], F32, name=f"summed{z}{t}")
+                nc.vector.tensor_tensor(
+                    summed[:], store_keys[z][t][:].indirect(key_list[:]), own_keys[z][:, t * I : (t + 1) * I], ADD
+                )
+                col = z * PACK + t
+                nc.scalar.activation(grouped[:, :, t], summed[:], COPY, scale=feat[:, col : col + 1])
+            nc.vector.quantize_mx(
+                out=key_codes[z][:].bitcast(E5M2X4),
+                scales=key_scales[z][:],
+                in_=grouped[:].rearrange("p i t -> p (i t)"),
+            )
+
+        half = LIST_COLS // ROW_TILES
+        scores = [psum.tile([P, I], F32, name=f"scores{h}") for h in range(ROW_TILES)]
+        for z in range(PASSES):
+            for h in range(ROW_TILES):
+                picked = keep.tile([P, P], U32, name=f"picked{z}{h}", align_bytes=64)
+                nc.vector.tensor_copy(picked[:], tok_words[z][:].indirect(tok_list[:, h * half : (h + 1) * half]))
+                nc.tensor.matmul_mx(
+                    out=scores[h][:],
+                    lhsT=picked[:].bitcast(E5M2X4),
+                    lhsT_scale=tok_scales[z][:, h * P : (h + 1) * P],
+                    rhs=key_codes[z][:].bitcast(E5M2X4),
+                    rhs_scale=key_scales[z][:],
+                    start=(z == 0),
+                    stop=(z == PASSES - 1),
+                )
+
+        for h in range(ROW_TILES):
+            biased = keep.tile([P, I], F32, name=f"biased{h}")
+            nc.vector.tensor_tensor(biased[:], scores[h][:], bias[:], ADD)
+            squashed = keep.tile([P, I], F32, name=f"squashed{h}")
+            nc.scalar.activation(squashed[:], biased[:], TANH)
+            picked_fac = keep.tile([P, I], F32, name=f"picked_fac{h}")
+            nc.scalar.activation(picked_fac[:], factors[h][:].indirect(fac_list[:]), COPY)
+            result = keep.tile([P, I], F32, name=f"result{h}")
+            nc.vector.tensor_tensor(result[:], squashed[:], picked_fac[:], MULT)
+            nc.sync.dma_start(out=out[h * P : (h + 1) * P, :], in_=result[:])

@@ -43,7 +43,7 @@ def tile_list_scores_picked_mixed_tabled_kernel(
             [keep.tile([P, V], F32, name=f"store_keys{z}{t}") for t in range(PACK)] for z in range(PASSES)
         ]
         own_keys = [keep.tile([P, PACK * I], F32, name=f"own_keys{z}") for z in range(PASSES)]
-        tok_words = [keep.tile([P, T], U32, name=f"tok_words{z}") for z in range(PASSES)]
+        tok_words = [keep.tile([P, T], U32, name=f"tok_words{z}", align_bytes=64) for z in range(PASSES)]
         factors = [keep.tile([P, C], F32, name=f"factors{h}") for h in range(ROW_TILES)]
         feat = keep.tile([P, PASSES * PACK], F32, name="feat")
         bias_col = keep.tile([P, 2], F32, name="bias_col")
@@ -53,26 +53,22 @@ def tile_list_scores_picked_mixed_tabled_kernel(
             out=feat[:].rearrange("p (z t) -> p z t", z=PASSES),
             in_=fi.rearrange("(z p t) o -> p z (t o)", z=PASSES, t=PACK),
         )
-        nc.vector.memset(tok_bytes[:].bitcast(I32), 0)
-
-        def load_scale_rows(q):
-            nc.sync.dma_start(
+        ident = keep.tile([P, P], F32, name="ident")
+        make_identity(nc, ident[:])
+        nc.gpsimd.memset(tok_bytes[:].bitcast(I32), 0)
+        for q in range(4):
+            nc.gpsimd.dma_start(
                 out=tok_bytes[32 * q : 32 * q + 4, :].bitcast(I32).rearrange("r (z c) -> r z c", z=PASSES),
                 in_=xt_scales[:, 4 * q : 4 * q + 4, :].bitcast(I32).rearrange("z r c -> r z c"),
             )
+        nc.gpsimd.dma_start(out=bias_col[:], in_=bi.rearrange("o (p u) -> p (o u)", u=2))
 
-        small = [lambda q=q: load_scale_rows(q) for q in range(4)] + [
-            lambda: nc.sync.dma_start(tok_list[:], offs),
-            lambda: nc.sync.dma_start(out=bias_col[:], in_=bi.rearrange("o (p u) -> p (o u)", u=2)),
-            lambda: nc.sync.dma_start(fac_list[:], offs3),
-        ]
+        lists = {(0, 0): (key_list, offs2), (0, 3): (tok_list, offs), (1, 2): (fac_list, offs3)}
         for z in range(PASSES):
             for t in range(PACK):
                 nc.sync.dma_start(out=store_keys[z][t][:], in_=kf_planes[z, t])
-                if z == 0 and t == 0:
-                    nc.sync.dma_start(key_list[:], offs2)
-                else:
-                    small[z * PACK + t - 1]()
+                if (z, t) in lists:
+                    nc.sync.dma_start(lists[z, t][0][:], lists[z, t][1])
                 if t == 0:
                     nc.sync.dma_start(out=own_keys[z][:], in_=ko_rows[z])
         for z in range(PASSES):
@@ -82,9 +78,6 @@ def tile_list_scores_picked_mixed_tabled_kernel(
             )
         for h in range(ROW_TILES):
             nc.sync.dma_start(out=factors[h][:], in_=tb[h * P : (h + 1) * P, :])
-
-        ident = keep.tile([P, P], F32, name="ident")
-        make_identity(nc, ident[:])
 
         bias_ps = psum.tile([P, 2, P], F32, name="bias_ps")
         for u in range(2):
@@ -96,46 +89,63 @@ def tile_list_scores_picked_mixed_tabled_kernel(
         for z in range(PASSES):
             nc.vector.tensor_copy(tok_scales[z][:], tok_bytes[:, z * T : (z + 1) * T].indirect(tok_list[:]))
 
-        key_codes = [keep.tile([P, I], U32, name=f"key_codes{z}", align_bytes=64) for z in range(PASSES)]
+        half = LIST_COLS // ROW_TILES
+        key_codes = {}
         key_scales = [keep.tile([P, I], U8, name=f"key_scales{z}", align_bytes=64) for z in range(PASSES)]
-        for z in range(PASSES):
-            grouped = keep.tile([P, I, PACK], BF16, name=f"grouped{z}", align_bytes=64)
+        grouped = [keep.tile([P, I, PACK], BF16, name=f"grouped{z}", align_bytes=64) for z in range(PASSES)]
+        scores = [psum.tile([P, I], F32, name=f"scores{h}") for h in range(ROW_TILES)]
+
+        def make_keys(z):
             for t in range(PACK):
                 summed = keep.tile([P, I], F32, name=f"summed{z}{t}")
                 nc.vector.tensor_tensor(
                     summed[:], store_keys[z][t][:].indirect(key_list[:]), own_keys[z][:, t * I : (t + 1) * I], ADD
                 )
                 col = z * PACK + t
-                nc.scalar.activation(grouped[:, :, t], summed[:], COPY, scale=feat[:, col : col + 1])
+                nc.scalar.activation(grouped[z][:, :, t], summed[:], COPY, scale=feat[:, col : col + 1])
+
+        def quantise_keys(z, tag):
+            key_codes[z] = keep.tile([P, I], U32, name=f"key_codes{z}", tag=tag, align_bytes=64)
             nc.vector.quantize_mx(
                 out=key_codes[z][:].bitcast(E5M2X4),
                 scales=key_scales[z][:],
-                in_=grouped[:].rearrange("p i t -> p (i t)"),
+                in_=grouped[z][:].rearrange("p i t -> p (i t)"),
             )
 
-        half = LIST_COLS // ROW_TILES
-        scores = [psum.tile([P, I], F32, name=f"scores{h}") for h in range(ROW_TILES)]
-        for z in range(PASSES):
-            for h in range(ROW_TILES):
-                picked = keep.tile([P, P], U32, name=f"picked{z}{h}", align_bytes=64)
-                nc.vector.tensor_copy(picked[:], tok_words[z][:].indirect(tok_list[:, h * half : (h + 1) * half]))
-                nc.tensor.matmul_mx(
-                    out=scores[h][:],
-                    lhsT=picked[:].bitcast(E5M2X4),
-                    lhsT_scale=tok_scales[z][:, h * P : (h + 1) * P],
-                    rhs=key_codes[z][:].bitcast(E5M2X4),
-                    rhs_scale=key_scales[z][:],
-                    start=(z == 0),
-                    stop=(z == PASSES - 1),
-                )
+        def pick_tokens(z, h):
+            picked = keep.tile([P, P], U32, name=f"picked{z}{h}", align_bytes=64)
+            nc.vector.tensor_copy(picked[:], tok_words[z][:].indirect(tok_list[:, h * half : (h + 1) * half]))
+            return picked
 
+        def multiply(z, h, picked):
+            nc.tensor.matmul_mx(
+                out=scores[h][:],
+                lhsT=picked[:].bitcast(E5M2X4),
+                lhsT_scale=tok_scales[z][:, h * P : (h + 1) * P],
+                rhs=key_codes[z][:].bitcast(E5M2X4),
+                rhs_scale=key_scales[z][:],
+                start=(z == 0),
+                stop=(z == PASSES - 1),
+            )
+
+        make_keys(0)
+        quantise_keys(0, "key_codes0")
+        make_keys(1)
+        for h in range(ROW_TILES):
+            multiply(0, h, pick_tokens(0, h))
+        quantise_keys(1, "tok_words0")
+        for h in range(ROW_TILES):
+            multiply(1, h, pick_tokens(1, h))
+
+        picked_fac = [keep.tile([P, I], F32, name=f"picked_fac{h}") for h in range(ROW_TILES)]
+        squashed = [keep.tile([P, I], F32, name=f"squashed{h}") for h in range(ROW_TILES)]
+        nc.scalar.activation(picked_fac[0][:], factors[0][:].indirect(fac_list[:]), COPY)
         for h in range(ROW_TILES):
             biased = keep.tile([P, I], F32, name=f"biased{h}")
             nc.vector.tensor_tensor(biased[:], scores[h][:], bias[:], ADD)
-            squashed = keep.tile([P, I], F32, name=f"squashed{h}")
-            nc.scalar.activation(squashed[:], biased[:], TANH)
-            picked_fac = keep.tile([P, I], F32, name=f"picked_fac{h}")
-            nc.scalar.activation(picked_fac[:], factors[h][:].indirect(fac_list[:]), COPY)
+            nc.scalar.activation(squashed[h][:], biased[:], TANH)
+        nc.vector.tensor_copy(picked_fac[1][:], factors[1][:].indirect(fac_list[:]))
+        for h in range(ROW_TILES):
             result = keep.tile([P, I], F32, name=f"result{h}")
-            nc.vector.tensor_tensor(result[:], squashed[:], picked_fac[:], MULT)
+            nc.vector.tensor_tensor(result[:], squashed[h][:], picked_fac[h][:], MULT)
             nc.sync.dma_start(out=out[h * P : (h + 1) * P, :], in_=result[:])

@@ -47,21 +47,21 @@ def tile_list_scores_picked_mixed_tabled_kernel(
         factors = [keep.tile([P, C], F32, name=f"factors{h}") for h in range(ROW_TILES)]
         feat = keep.tile([P, PASSES * PACK], F32, name="feat")
         bias_col = keep.tile([P, 2], F32, name="bias_col")
-        tok_bytes = keep.tile([P, PASSES * T], U8, name="tok_bytes")
+        tok_bytes = keep.tile([P, PASSES * T], U8, name="tok_bytes", align_bytes=64)
 
         nc.scalar.dma_start(
             out=feat[:].rearrange("p (z t) -> p z t", z=PASSES),
             in_=fi.rearrange("(z p t) o -> p z (t o)", z=PASSES, t=PACK),
         )
+        nc.scalar.dma_start(out=bias_col[:], in_=bi.rearrange("o (p u) -> p (o u)", u=2))
         ident = keep.tile([P, P], F32, name="ident")
         make_identity(nc, ident[:])
-        nc.gpsimd.memset(tok_bytes[:].bitcast(I32), 0)
+        nc.vector.memset(tok_bytes[:].bitcast(I32), 0)
         for q in range(4):
-            nc.gpsimd.dma_start(
+            nc.scalar.dma_start(
                 out=tok_bytes[32 * q : 32 * q + 4, :].bitcast(I32).rearrange("r (z c) -> r z c", z=PASSES),
                 in_=xt_scales[:, 4 * q : 4 * q + 4, :].bitcast(I32).rearrange("z r c -> r z c"),
             )
-        nc.gpsimd.dma_start(out=bias_col[:], in_=bi.rearrange("o (p u) -> p (o u)", u=2))
 
         lists = {(0, 0): (key_list, offs2), (0, 3): (tok_list, offs), (1, 2): (fac_list, offs3)}
         for z in range(PASSES):
@@ -97,7 +97,8 @@ def tile_list_scores_picked_mixed_tabled_kernel(
 
         def make_keys(z):
             for t in range(PACK):
-                summed = keep.tile([P, I], F32, name=f"summed{z}{t}")
+                tag = "tok_bytes" if (z, t) == (1, 0) else f"summed{z}{t}"
+                summed = keep.tile([P, I], F32, name=f"summed{z}{t}", tag=tag, align_bytes=64)
                 nc.vector.tensor_tensor(
                     summed[:], store_keys[z][t][:].indirect(key_list[:]), own_keys[z][:, t * I : (t + 1) * I], ADD
                 )
@@ -113,7 +114,8 @@ def tile_list_scores_picked_mixed_tabled_kernel(
             )
 
         def pick_tokens(z, h):
-            picked = keep.tile([P, P], U32, name=f"picked{z}{h}", align_bytes=64)
+            tag = {(0, 0): "summed12", (1, 0): "grouped1"}.get((z, h), f"picked{z}{h}")
+            picked = keep.tile([P, P], U32, name=f"picked{z}{h}", tag=tag, align_bytes=64)
             nc.vector.tensor_copy(picked[:], tok_words[z][:].indirect(tok_list[:, h * half : (h + 1) * half]))
             return picked
 
@@ -137,7 +139,10 @@ def tile_list_scores_picked_mixed_tabled_kernel(
         for h in range(ROW_TILES):
             multiply(1, h, pick_tokens(1, h))
 
-        picked_fac = [keep.tile([P, I], F32, name=f"picked_fac{h}") for h in range(ROW_TILES)]
+        picked_fac = [
+            keep.tile([P, I], F32, name=f"picked_fac{h}", tag=tag, align_bytes=64)
+            for h, tag in enumerate(("summed13", "picked11"))
+        ]
         squashed = [keep.tile([P, I], F32, name=f"squashed{h}") for h in range(ROW_TILES)]
         nc.scalar.activation(picked_fac[0][:], factors[0][:].indirect(fac_list[:]), COPY)
         for h in range(ROW_TILES):

@@ -21,8 +21,13 @@ TANH = mybir.ActivationFunctionType.Tanh
 P = 128
 PACK = 4
 PASSES = K // (P * PACK)
+QUADRANT = 32
+SCALE_ROWS = 4
 ROW_TILES = J // P
+BIAS_RUN = I // P
 LIST_COLS = J // 16
+TILE_LIST_COLS = P // 16
+MX_ALIGN = 64
 
 
 def tile_list_scores_picked_mixed_tabled_kernel(
@@ -42,35 +47,48 @@ def tile_list_scores_picked_mixed_tabled_kernel(
         store_keys = [
             [keep.tile([P, V], F32, name=f"store_keys{z}{t}") for t in range(PACK)] for z in range(PASSES)
         ]
-        own_keys = [keep.tile([P, PACK * I], F32, name=f"own_keys{z}") for z in range(PASSES)]
-        tok_words = [keep.tile([P, T], U32, name=f"tok_words{z}", align_bytes=64) for z in range(PASSES)]
+        own_keys = [
+            keep.tile([P, PACK * I], F32, name=f"own_keys{z}", align_bytes=MX_ALIGN) for z in range(PASSES)
+        ]
+        tok_words = [keep.tile([P, T], U32, name=f"tok_words{z}", align_bytes=MX_ALIGN) for z in range(PASSES)]
         factors = [keep.tile([P, C], F32, name=f"factors{h}") for h in range(ROW_TILES)]
-        feat = keep.tile([P, PASSES * PACK], F32, name="feat")
-        bias_col = keep.tile([P, 2], F32, name="bias_col")
-        tok_bytes = keep.tile([P, PASSES * T], U8, name="tok_bytes", align_bytes=64)
+        feat = keep.tile([P, PASSES, 2 * PACK], F32, name="feat")
+        bias_col = keep.tile([P, BIAS_RUN], F32, name="bias_col")
+        tok_bytes = keep.tile([P, PASSES * T], U8, name="tok_bytes", align_bytes=MX_ALIGN)
 
         nc.scalar.dma_start(
-            out=feat[:].rearrange("p (z t) -> p z t", z=PASSES),
+            out=feat[:, :, 0:PACK],
             in_=fi.rearrange("(z p t) o -> p z (t o)", z=PASSES, t=PACK),
         )
-        nc.scalar.dma_start(out=bias_col[:], in_=bi.rearrange("o (p u) -> p (o u)", u=2))
         ident = keep.tile([P, P], F32, name="ident")
         make_identity(nc, ident[:])
         nc.vector.memset(tok_bytes[:].bitcast(I32), 0)
-        for q in range(4):
-            nc.scalar.dma_start(
-                out=tok_bytes[32 * q : 32 * q + 4, :].bitcast(I32).rearrange("r (z c) -> r z c", z=PASSES),
-                in_=xt_scales[:, 4 * q : 4 * q + 4, :].bitcast(I32).rearrange("z r c -> r z c"),
+
+        def load_plane(z, t):
+            nc.sync.dma_start(out=store_keys[z][t][:], in_=kf_planes[z, t])
+
+        def load_scale_rows(q):
+            first = QUADRANT * q
+            nc.sync.dma_start(
+                out=tok_bytes[first : first + SCALE_ROWS, :].bitcast(I32).rearrange("r (z c) -> r z c", z=PASSES),
+                in_=xt_scales[:, SCALE_ROWS * q : SCALE_ROWS * (q + 1), :].bitcast(I32).rearrange("z r c -> r z c"),
             )
 
-        lists = {(0, 0): (key_list, offs2), (0, 3): (tok_list, offs), (1, 2): (fac_list, offs3)}
-        for z in range(PASSES):
-            for t in range(PACK):
-                nc.sync.dma_start(out=store_keys[z][t][:], in_=kf_planes[z, t])
-                if (z, t) in lists:
-                    nc.sync.dma_start(lists[z, t][0][:], lists[z, t][1])
-                if t == 0:
-                    nc.sync.dma_start(out=own_keys[z][:], in_=ko_rows[z])
+        load_plane(0, 0)
+        nc.sync.dma_start(key_list[:], offs2)
+        nc.sync.dma_start(out=own_keys[0][:], in_=ko_rows[0])
+        load_scale_rows(0)
+        for t in range(1, PACK):
+            load_plane(0, t)
+            load_scale_rows(t)
+        nc.sync.dma_start(tok_list[:], offs)
+        load_plane(1, 0)
+        nc.sync.dma_start(out=own_keys[1][:], in_=ko_rows[1])
+        nc.sync.dma_start(out=bias_col[:], in_=bi.rearrange("o (p u) -> p (o u)", u=BIAS_RUN))
+        load_plane(1, 1)
+        nc.sync.dma_start(fac_list[:], offs3)
+        load_plane(1, 2)
+        load_plane(1, 3)
         for z in range(PASSES):
             nc.sync.dma_start(
                 out=tok_words[z][:].bitcast(I32),
@@ -79,69 +97,66 @@ def tile_list_scores_picked_mixed_tabled_kernel(
         for h in range(ROW_TILES):
             nc.sync.dma_start(out=factors[h][:], in_=tb[h * P : (h + 1) * P, :])
 
-        bias_ps = psum.tile([P, 2, P], F32, name="bias_ps")
-        for u in range(2):
+        bias_ps = psum.tile([P, BIAS_RUN, P], F32, name="bias_ps")
+        for u in range(BIAS_RUN):
             nc.tensor.transpose(bias_ps[:, u, :], bias_col[:, u : u + 1].to_broadcast([P, P]), ident[:])
         bias = keep.tile([P, I], F32, name="bias")
-        nc.scalar.copy(out=bias[:].rearrange("m (p u) -> m p u", u=2), in_=bias_ps[:].rearrange("m u p -> m p u"))
+        nc.scalar.copy(
+            out=bias[:].rearrange("m (p u) -> m p u", u=BIAS_RUN), in_=bias_ps[:].rearrange("m u p -> m p u")
+        )
 
-        tok_scales = [keep.tile([P, J], U8, name=f"tok_scales{z}", align_bytes=64) for z in range(PASSES)]
+        tok_scales = [keep.tile([P, J], U8, name=f"tok_scales{z}", align_bytes=MX_ALIGN) for z in range(PASSES)]
         for z in range(PASSES):
             nc.vector.tensor_copy(tok_scales[z][:], tok_bytes[:, z * T : (z + 1) * T].indirect(tok_list[:]))
 
-        half = LIST_COLS // ROW_TILES
         key_codes = {}
-        key_scales = [keep.tile([P, I], U8, name=f"key_scales{z}", align_bytes=64) for z in range(PASSES)]
-        grouped = [keep.tile([P, I, PACK], BF16, name=f"grouped{z}", align_bytes=64) for z in range(PASSES)]
+        key_scales = [keep.tile([P, I], U8, name=f"key_scales{z}", align_bytes=MX_ALIGN) for z in range(PASSES)]
+        grouped = [keep.tile([P, I, PACK], BF16, name=f"grouped{z}", align_bytes=MX_ALIGN) for z in range(PASSES)]
         scores = [psum.tile([P, I], F32, name=f"scores{h}") for h in range(ROW_TILES)]
 
         def make_keys(z):
+            summed = keep.tile([P, PACK * I], F32, name=f"summed{z}", align_bytes=MX_ALIGN)
             for t in range(PACK):
-                tag = "tok_bytes" if (z, t) == (1, 0) else f"summed{z}{t}"
-                summed = keep.tile([P, I], F32, name=f"summed{z}{t}", tag=tag, align_bytes=64)
+                cols = slice(t * I, (t + 1) * I)
                 nc.vector.tensor_tensor(
-                    summed[:], store_keys[z][t][:].indirect(key_list[:]), own_keys[z][:, t * I : (t + 1) * I], ADD
+                    summed[:, cols], store_keys[z][t][:].indirect(key_list[:]), own_keys[z][:, cols], ADD
                 )
-                col = z * PACK + t
-                nc.scalar.activation(grouped[z][:, :, t], summed[:], COPY, scale=feat[:, col : col + 1])
+                nc.scalar.activation(grouped[z][:, :, t], summed[:, cols], COPY, scale=feat[:, z, t : t + 1])
 
-        def quantise_keys(z, tag):
-            key_codes[z] = keep.tile([P, I], U32, name=f"key_codes{z}", tag=tag, align_bytes=64)
+        def quantise_keys(z, after):
+            key_codes[z] = keep.tile([P, I], U32, name=f"key_codes{z}", tag=after, align_bytes=MX_ALIGN)
             nc.vector.quantize_mx(
                 out=key_codes[z][:].bitcast(E5M2X4),
                 scales=key_scales[z][:],
                 in_=grouped[z][:].rearrange("p i t -> p (i t)"),
             )
 
-        def pick_tokens(z, h):
-            tag = {(0, 0): "summed12", (1, 0): "grouped1"}.get((z, h), f"picked{z}{h}")
-            picked = keep.tile([P, P], U32, name=f"picked{z}{h}", tag=tag, align_bytes=64)
-            nc.vector.tensor_copy(picked[:], tok_words[z][:].indirect(tok_list[:, h * half : (h + 1) * half]))
-            return picked
-
-        def multiply(z, h, picked):
-            nc.tensor.matmul_mx(
-                out=scores[h][:],
-                lhsT=picked[:].bitcast(E5M2X4),
-                lhsT_scale=tok_scales[z][:, h * P : (h + 1) * P],
-                rhs=key_codes[z][:].bitcast(E5M2X4),
-                rhs_scale=key_scales[z][:],
-                start=(z == 0),
-                stop=(z == PASSES - 1),
-            )
+        def pick_and_multiply(z, after):
+            picked = keep.tile([P, J], U32, name=f"picked{z}", tag=after, align_bytes=MX_ALIGN)
+            for h in range(ROW_TILES):
+                rows = slice(h * P, (h + 1) * P)
+                entries = tok_list[:, h * TILE_LIST_COLS : (h + 1) * TILE_LIST_COLS]
+                nc.vector.tensor_copy(picked[:, rows], tok_words[z][:].indirect(entries))
+                nc.tensor.matmul_mx(
+                    out=scores[h][:],
+                    lhsT=picked[:, rows].bitcast(E5M2X4),
+                    lhsT_scale=tok_scales[z][:, rows],
+                    rhs=key_codes[z][:].bitcast(E5M2X4),
+                    rhs_scale=key_scales[z][:],
+                    start=(z == 0),
+                    stop=(z == PASSES - 1),
+                )
 
         make_keys(0)
-        quantise_keys(0, "key_codes0")
+        quantise_keys(0, after="tok_bytes")
         make_keys(1)
-        for h in range(ROW_TILES):
-            multiply(0, h, pick_tokens(0, h))
-        quantise_keys(1, "tok_words0")
-        for h in range(ROW_TILES):
-            multiply(1, h, pick_tokens(1, h))
+        pick_and_multiply(0, after="own_keys1")
+        quantise_keys(1, after="tok_words0")
+        pick_and_multiply(1, after="grouped1")
 
         picked_fac = [
-            keep.tile([P, I], F32, name=f"picked_fac{h}", tag=tag, align_bytes=64)
-            for h, tag in enumerate(("summed13", "picked11"))
+            keep.tile([P, I], F32, name=f"picked_fac{h}", tag=after, align_bytes=MX_ALIGN)
+            for h, after in enumerate(("summed1", "grouped1"))
         ]
         squashed = [keep.tile([P, I], F32, name=f"squashed{h}") for h in range(ROW_TILES)]
         nc.scalar.activation(picked_fac[0][:], factors[0][:].indirect(fac_list[:]), COPY)

from contextlib import ExitStack

import concourse.mybir as mybir
from concourse.masks import make_identity

K, T, J, I, V, C = 1024, 1024, 256, 256, 1024, 512
FLOPS = 2 * K * J * I

F32 = mybir.dt.float32
BF16 = mybir.dt.bfloat16
I32 = mybir.dt.int32
U32 = mybir.dt.uint32
U16 = mybir.dt.uint16
U8 = mybir.dt.uint8
E5M2X4 = mybir.dt.float8_e5m2_x4
ADD = mybir.AluOpType.add
MULT = mybir.AluOpType.mult
COPY = mybir.ActivationFunctionType.Copy
TANH = mybir.ActivationFunctionType.Tanh

P = 128
PACK = 4
PASSES = K // (P * PACK)
QUADRANT = 32
SCALE_ROWS = 4
ROW_TILES = J // P
BIAS_RUN = I // P
LIST_COLS = J // 16
TILE_LIST_COLS = P // 16
MX_ALIGN = 64


def tile_list_scores_picked_mixed_tabled_kernel(
    tc, xt_words, xt_scales, kf, ko, fi, bi, tb, offs, offs2, offs3, out
):
    nc = tc.nc
    with ExitStack() as ctx:
        keep = ctx.enter_context(tc.tile_pool(name="keep", bufs=1))
        psum = ctx.enter_context(tc.psum_pool(name="psum", bufs=1))

        tok_list = keep.tile([P, LIST_COLS], U16, name="tok_list")
        key_list = keep.tile([P, LIST_COLS], U16, name="key_list")
        fac_list = keep.tile([P, LIST_COLS], U16, name="fac_list")

        kf_planes = kf.rearrange("(z p t) v -> z t p v", z=PASSES, t=PACK)
        ko_rows = ko.rearrange("(z p t) i -> z p (t i)", z=PASSES, t=PACK)
        store_keys = [
            [keep.tile([P, V], F32, name=f"store_keys{z}{t}") for t in range(PACK)] for z in range(PASSES)
        ]
        own_keys = [
            keep.tile([P, PACK * I], F32, name=f"own_keys{z}", align_bytes=MX_ALIGN) for z in range(PASSES)
        ]
        tok_words = [keep.tile([P, T], U32, name=f"tok_words{z}", align_bytes=MX_ALIGN) for z in range(PASSES)]
        factors = [keep.tile([P, C], F32, name=f"factors{h}") for h in range(ROW_TILES)]
        feat = keep.tile([P, PASSES, 2 * PACK], F32, name="feat")
        bias_col = keep.tile([P, BIAS_RUN], F32, name="bias_col")
        tok_bytes = keep.tile([P, PASSES * T], U8, name="tok_bytes", align_bytes=MX_ALIGN)

        nc.scalar.dma_start(
            out=feat[:, :, 0:PACK],
            in_=fi.rearrange("(z p t) o -> p z (t o)", z=PASSES, t=PACK),
        )
        ident = keep.tile([P, P], F32, name="ident")
        make_identity(nc, ident[:])
        nc.vector.memset(tok_bytes[:].bitcast(I32), 0)

        def load_plane(z, t):
            nc.sync.dma_start(out=store_keys[z][t][:], in_=kf_planes[z, t])

        def load_scale_rows(q):
            first = QUADRANT * q
            nc.sync.dma_start(
                out=tok_bytes[first : first + SCALE_ROWS, :].bitcast(I32).rearrange("r (z c) -> r z c", z=PASSES),
                in_=xt_scales[:, SCALE_ROWS * q : SCALE_ROWS * (q + 1), :].bitcast(I32).rearrange("z r c -> r z c"),
            )

        load_plane(0, 0)
        nc.sync.dma_start(key_list[:], offs2)
        nc.sync.dma_start(out=own_keys[0][:], in_=ko_rows[0])
        load_scale_rows(0)
        for t in range(1, PACK):
            load_plane(0, t)
            load_scale_rows(t)
        nc.sync.dma_start(tok_list[:], offs)
        load_plane(1, 0)
        nc.sync.dma_start(out=own_keys[1][:], in_=ko_rows[1])
        nc.sync.dma_start(out=bias_col[:], in_=bi.rearrange("o (p u) -> p (o u)", u=BIAS_RUN))
        load_plane(1, 1)
        nc.sync.dma_start(fac_list[:], offs3)
        load_plane(1, 2)
        load_plane(1, 3)
        for z in range(PASSES):
            nc.sync.dma_start(
                out=tok_words[z][:].bitcast(I32),
                in_=xt_words[z].rearrange("p c r -> p (c r)").bitcast(I32),
            )
        for h in range(ROW_TILES):
            nc.sync.dma_start(out=factors[h][:], in_=tb[h * P : (h + 1) * P, :])

        bias_ps = psum.tile([P, BIAS_RUN, P], F32, name="bias_ps")
        for u in range(BIAS_RUN):
            nc.tensor.transpose(bias_ps[:, u, :], bias_col[:, u : u + 1].to_broadcast([P, P]), ident[:])
        bias = keep.tile([P, I], F32, name="bias")
        nc.scalar.copy(
            out=bias[:].rearrange("m (p u) -> m p u", u=BIAS_RUN), in_=bias_ps[:].rearrange("m u p -> m p u")
        )

        tok_scales = [keep.tile([P, J], U8, name=f"tok_scales{z}", align_bytes=MX_ALIGN) for z in range(PASSES)]
        for z in range(PASSES):
            nc.vector.tensor_copy(tok_scales[z][:], tok_bytes[:, z * T : (z + 1) * T].indirect(tok_list[:]))

        key_codes = {}
        key_scales = [keep.tile([P, I], U8, name=f"key_scales{z}", align_bytes=MX_ALIGN) for z in range(PASSES)]
        grouped = [keep.tile([P, I, PACK], BF16, name=f"grouped{z}", align_bytes=MX_ALIGN) for z in range(PASSES)]
        scores = [psum.tile([P, I], F32, name=f"scores{h}") for h in range(ROW_TILES)]

        def make_keys(z):
            summed = keep.tile([P, PACK * I], F32, name=f"summed{z}", align_bytes=MX_ALIGN)
            for t in range(PACK):
                cols = slice(t * I, (t + 1) * I)
                nc.vector.tensor_tensor(
                    summed[:, cols], store_keys[z][t][:].indirect(key_list[:]), own_keys[z][:, cols], ADD
                )
                nc.scalar.activation(grouped[z][:, :, t], summed[:, cols], COPY, scale=feat[:, z, t : t + 1])

        def quantise_keys(z, after):
            key_codes[z] = keep.tile([P, I], U32, name=f"key_codes{z}", tag=after, align_bytes=MX_ALIGN)
            nc.vector.quantize_mx(
                out=key_codes[z][:].bitcast(E5M2X4),
                scales=key_scales[z][:],
                in_=grouped[z][:].rearrange("p i t -> p (i t)"),
            )

        def pick_and_multiply(z, after):
            picked = keep.tile([P, J], U32, name=f"picked{z}", tag=after, align_bytes=MX_ALIGN)
            for h in range(ROW_TILES):
                rows = slice(h * P, (h + 1) * P)
                entries = tok_list[:, h * TILE_LIST_COLS : (h + 1) * TILE_LIST_COLS]
                nc.vector.tensor_copy(picked[:, rows], tok_words[z][:].indirect(entries))
                nc.tensor.matmul_mx(
                    out=scores[h][:],
                    lhsT=picked[:, rows].bitcast(E5M2X4),
                    lhsT_scale=tok_scales[z][:, rows],
                    rhs=key_codes[z][:].bitcast(E5M2X4),
                    rhs_scale=key_scales[z][:],
                    start=(z == 0),
                    stop=(z == PASSES - 1),
                )

        make_keys(0)
        quantise_keys(0, after="tok_bytes")
        make_keys(1)
        pick_and_multiply(0, after="own_keys1")
        quantise_keys(1, after="tok_words0")
        pick_and_multiply(1, after="grouped1")

        picked_fac = [
            keep.tile([P, I], F32, name=f"picked_fac{h}", tag=after, align_bytes=MX_ALIGN)
            for h, after in enumerate(("summed1", "grouped1"))
        ]
        squashed = [keep.tile([P, I], F32, name=f"squashed{h}") for h in range(ROW_TILES)]
        nc.scalar.activation(picked_fac[0][:], factors[0][:].indirect(fac_list[:]), COPY)
        for h in range(ROW_TILES):
            biased = keep.tile([P, I], F32, name=f"biased{h}")
            nc.vector.tensor_tensor(biased[:], scores[h][:], bias[:], ADD)
            nc.scalar.activation(squashed[h][:], biased[:], TANH)
        nc.vector.tensor_copy(picked_fac[1][:], factors[1][:].indirect(fac_list[:]))
        for h in range(ROW_TILES):
            result = keep.tile([P, I], F32, name=f"result{h}")
            nc.vector.tensor_tensor(result[:], squashed[h][:], picked_fac[h][:], MULT)
            nc.sync.dma_start(out=out[h * P : (h + 1) * P, :], in_=result[:])
